import numpy as np
import ml_dtypes


def mxq(x, axis, fmt="e4m3"):
    dtype, down = {"e4m3": (ml_dtypes.float8_e4m3fn, 7), "e5m2": (ml_dtypes.float8_e5m2, 14)}[fmt]
    v = np.moveaxis(np.asarray(x, np.float32).astype(ml_dtypes.bfloat16).astype(np.float64), axis, -1)
    blocks = v.reshape(v.shape[:-1] + (-1, 32))
    amax = np.abs(blocks).max(-1, keepdims=True)
    byte = np.maximum(np.where(amax > 0, np.frexp(amax)[1] - 1 + 127, 0) - down, 1)
    scale = np.exp2(byte - 127.0)
    codes = (blocks / scale).astype(np.float32).astype(dtype).astype(np.float64)
    return np.moveaxis((codes * scale).reshape(v.shape), -1, axis)


WIDE = False


def mx_kscale(k):
    if not WIDE:
        return np.ones(k)
    levels = np.array([10, -10, 5, -5, 0])
    if k % 512:
        return np.exp2(np.random.permutation(np.resize(levels, k // 32))).repeat(32)
    a = np.empty((k // 512, 16))
    for p in range(k // 512):
        a[p, :8] = np.random.permutation(np.resize(levels, 8))
        for g in range(8):
            far = levels[np.abs(levels - a[p, g]) >= 10]
            a[p, g + 8] = far[np.random.randint(len(far))]
    return np.exp2(a.ravel()).repeat(32)


def f64(x):
    return np.asarray(x).astype(np.float64)


def striped8(idx):
    return np.asarray(idx).reshape(8, -1, 16).transpose(0, 2, 1).reshape(128, -1).astype(np.uint16)


def unstriped8(offs):
    return offs.reshape(8, 16, -1).transpose(0, 2, 1).reshape(8, -1).astype(np.int64)


def pick8(x, idx, run):
    r = np.arange(len(x))
    return x[r[:, None], idx[r % (8 * run) // run]]


E2M1 = np.array([0.0, 0.5, 1.0, 1.5, 2.0, 3.0, 4.0, 6.0, -0.0, -0.5, -1.0, -1.5, -2.0, -3.0, -4.0, -6.0])


def pack_weight(w, fmt):
    k, n = w.shape
    w = f64(np.asarray(w, np.float32).astype(ml_dtypes.bfloat16)).reshape(k // 32, 32, n)
    amax = np.abs(w).max(1)
    if fmt == "e4m3":
        byte = np.frexp(amax)[1] - 1 + 127 - 7
    else:
        mant, ex = np.frexp(amax / 6.0)
        byte = np.where(mant > 0.5, ex, ex - 1) + 127
    byte = np.clip(np.where(amax > 0, byte, 1), 1, 254)
    scaled = (w * np.exp2(127.0 - byte)[:, None, :]).reshape(k, n).astype(np.float32)
    by_word = np.ascontiguousarray(scaled.reshape(k // 512, 128, 4, n).transpose(0, 1, 3, 2))
    if fmt == "e4m3":
        words = by_word.astype(ml_dtypes.float8_e4m3fn).view(np.uint8)
    else:
        c = by_word.astype(ml_dtypes.float4_e2m1fn).view(np.uint8) & 0xF
        words = (c[..., 0::2] | (c[..., 1::2] << 4)).reshape(k // 512, 128, 2 * n)
    return np.ascontiguousarray(words), np.ascontiguousarray(byte.astype(np.uint8).reshape(k // 512, 16, n))


def unpack_weight(words, scales, fmt):
    g, _, n = scales.shape
    words = np.ascontiguousarray(words).reshape(g, 128, n, -1)
    if fmt == "e4m3":
        vals = words.view(ml_dtypes.float8_e4m3fn).astype(np.float64)
    else:
        nib = np.empty((g, 128, n, 4), np.uint8)
        nib[..., 0::2] = words & 0xF
        nib[..., 1::2] = words >> 4
        vals = E2M1[nib]
    vals = vals * np.repeat(np.exp2(scales.astype(np.float64) - 127.0), 8, axis=1)[..., None]
    return vals.transpose(0, 1, 3, 2).reshape(g * 512, n)


D, T, I, Q = 512, 1024, 512, 128


def setup_inputs():
    n = np.random.standard_normal
    idx = np.stack([np.random.permutation(T)[:I] for _ in range(8)])
    idx2 = np.stack([np.random.permutation(T)[:I] for _ in range(8)])
    idx3 = np.stack([np.random.permutation(T)[:I] for _ in range(8)])
    idx4 = np.stack([np.random.permutation(T)[:I] for _ in range(8)])
    fd = mx_kscale(D)
    keysp = pack_weight(n((D, T)) / fd[:, None], "e4m3")
    return {
        "query": (n((D, Q)) * 1.2 / np.sqrt(D) * fd[:, None]).astype(np.float32),
        "keys_words": keysp[0],
        "keys_scales": keysp[1],
        "lam": (np.random.uniform(0.8, 1.8, (Q, 1))).astype(np.float32),
        "old": (1.0 * n((Q, T))).astype(np.float32),
        "offs": striped8(idx),
        "offs2": striped8(idx2),
        "offs3": striped8(idx3),
        "offs4": striped8(idx4),
    }


def reference(query, keys_words, keys_scales, lam, old, offs, offs2, offs3, offs4):
    idx = unstriped8(offs)
    idx2 = unstriped8(offs2)
    idx3 = unstriped8(offs3)
    idx4 = unstriped8(offs4)
    keysu = unpack_weight(keys_words, keys_scales, "e4m3")
    queryq = mxq(f64(query), 0, "e4m3")
    a = queryq.T @ keysu
    lo2 = np.minimum(pick8(a, idx, 16), pick8(a, idx2, 16))
    hi2 = np.maximum(pick8(a, idx, 16), pick8(a, idx2, 16))
    w = np.maximum(lo2, np.minimum(hi2, pick8(a, idx3, 16))) * f64(lam)
    f1 = np.zeros((Q, T))
    f1[np.arange(Q)[:, None], idx[np.arange(Q) % 128 // 16]] = w
    f2 = f1 + f64(old)
    y = pick8(f2, idx4, 16)
    return y

@@ -1,0 +1,136 @@
+from contextlib import ExitStack
+
+import concourse.mybir as mybir
+
+F32 = mybir.dt.float32
+BF16 = mybir.dt.bfloat16
+I32 = mybir.dt.int32
+U32 = mybir.dt.uint32
+U16 = mybir.dt.uint16
+U8 = mybir.dt.uint8
+FP8X4 = mybir.dt.float8_e4m3fn_x4
+ALU = mybir.AluOpType
+COPY = mybir.ActivationFunctionType.Copy
+
+D, T, SLOTS, Q = 512, 1024, 512, 128
+P = 128
+PACK = 4
+HALF = SLOTS // 2
+LIST_HALF = HALF // 16
+N_MM = 256
+
+FLOPS = 2 * D * T * Q
+
+
+def tile_attend_middle_lean_through_heads_kernel(
+    tc, query, keys_words, keys_scales, lam, old, offs, offs2, offs3, offs4, out
+):
+    nc = tc.nc
+    with ExitStack() as ctx:
+        keep = ctx.enter_context(tc.tile_pool(name="keep", bufs=1))
+        psum = ctx.enter_context(tc.psum_pool(name="psum", bufs=1))
+
+        k_scales = keep.tile([P, T], U8, name="k_scales", align_bytes=64)
+        nc.vector.memset(k_scales[:].bitcast(I32), 0)
+
+        q_raw = keep.tile([P, PACK, Q], F32, name="q_raw")
+        nc.sync.dma_start(out=q_raw[:], in_=query.rearrange("(p j) q -> p j q", j=PACK))
+
+        words_hbm = keys_words[0].rearrange("p t r -> p (t r)").bitcast(I32)
+        scales_hbm = keys_scales[0].bitcast(I32)
+        k_words = []
+        for h in range(2):
+            w = keep.tile([P, T // 2], I32, name="k_words%d" % h, align_bytes=64)
+            nc.sync.dma_start(out=w[:], in_=words_hbm[:, h * (T // 2) : (h + 1) * (T // 2)])
+            k_words.append(w)
+            if h == 0:
+                for quad in range(4):
+                    nc.sync.dma_start(
+                        out=k_scales[32 * quad : 32 * quad + 4, :].bitcast(I32),
+                        in_=scales_hbm[4 * quad : 4 * quad + 4, :],
+                    )
+
+        lists = []
+        for n, src in enumerate((offs, offs2, offs3)):
+            lst = keep.tile([P, SLOTS // 16], U16, name="list%d" % n)
+            nc.sync.dma_start(lst[:], src)
+            lists.append(lst)
+        lam_col = keep.tile([P, 1], F32, name="lam_col")
+        nc.sync.dma_start(out=lam_col[:], in_=lam)
+        list_out = keep.tile([P, SLOTS // 16], U16, name="list_out")
+        nc.sync.dma_start(list_out[:], offs4)
+        old_sb = keep.tile([P, T], F32, name="old_sb")
+        nc.sync.dma_start(out=old_sb[:], in_=old)
+
+        f1 = keep.tile([P, T], F32, name="f1")
+        nc.vector.memset(f1[:], 0.0)
+
+        q_bf = keep.tile([P, Q, PACK], BF16, name="q_bf", align_bytes=64)
+        nc.vector.tensor_copy(
+            out=q_bf[:].rearrange("p (c i) j -> p c j i", i=4),
+            in_=q_raw[:].rearrange("p j (c i) -> p c j i", i=4),
+        )
+        q_codes = keep.tile([P, Q], U32, name="q_codes", align_bytes=64)
+        q_scales = keep.tile([P, Q], U8, name="q_scales", align_bytes=64)
+        nc.vector.quantize_mx(
+            out=q_codes[:].bitcast(FP8X4),
+            scales=q_scales[:],
+            in_=q_bf[:].rearrange("p q j -> p (q j)"),
+        )
+
+        a = keep.tile([P, T], F32, name="a")
+        for c in range(T // N_MM):
+            h, c0 = divmod(c * N_MM, T // 2)
+            cols = slice(c * N_MM, (c + 1) * N_MM)
+            bank = psum.tile([P, N_MM], F32, name="bank%d" % c)
+            nc.tensor.matmul_mx(
+                out=bank[:],
+                lhsT=q_codes[:].bitcast(FP8X4),
+                lhsT_scale=q_scales[:],
+                rhs=k_words[h][:, c0 : c0 + N_MM].bitcast(FP8X4),
+                rhs_scale=k_scales[:, cols],
+                start=True,
+                stop=True,
+            )
+            if c % 2 == 0:
+                nc.scalar.copy(out=a[:, cols], in_=bank[:])
+            else:
+                nc.vector.tensor_copy(out=a[:, cols], in_=bank[:])
+
+        lam_wide = keep.tile([P, SLOTS], F32, name="lam_wide")
+        nc.gpsimd.tensor_copy(out=lam_wide[:], in_=lam_col[:].to_broadcast([P, SLOTS]))
+
+        def half_of(lst, h):
+            return lst[:, h * LIST_HALF : (h + 1) * LIST_HALF]
+
+        got = {}
+        for h in range(2):
+            for n in range(3):
+                g = keep.tile([P, HALF], F32, name="got%d_%d" % (h, n))
+                if n == 0:
+                    nc.vector.tensor_copy(g[:], a[:].indirect(half_of(lists[n], h)))
+                else:
+                    nc.scalar.activation(g[:], a[:].indirect(half_of(lists[n], h)), COPY)
+                got[h, n] = g
+        lo, cut = [], []
+        for h in range(2):
+            hi = keep.tile([P, HALF], F32, name="hi%d" % h)
+            lo.append(keep.tile([P, HALF], F32, name="lo%d" % h))
+            cut.append(keep.tile([P, HALF], F32, name="cut%d" % h))
+            nc.vector.tensor_tensor(hi[:], got[h, 0][:], got[h, 1][:], ALU.max)
+            nc.vector.tensor_tensor(lo[h][:], got[h, 0][:], got[h, 1][:], ALU.min)
+            nc.vector.tensor_tensor(cut[h][:], hi[:], got[h, 2][:], ALU.min)
+        med = keep.tile([P, SLOTS], F32, name="med")
+        for h in range(2):
+            nc.vector.tensor_tensor(med[:, h * HALF : (h + 1) * HALF], lo[h][:], cut[h][:], ALU.max)
+        nc.vector.tensor_tensor(f1[:].indirect(lists[0][:]), med[:], lam_wide[:], ALU.mult)
+
+        f2 = keep.tile([P, T], F32, name="f2")
+        nc.vector.tensor_tensor(f2[:], f1[:], old_sb[:], ALU.add)
+
+        res0 = keep.tile([P, HALF], F32, name="res0")
+        res1 = keep.tile([P, HALF], F32, name="res1")
+        nc.vector.tensor_copy(res0[:], f2[:].indirect(half_of(list_out, 0)))
+        nc.scalar.activation(res1[:], f2[:].indirect(half_of(list_out, 1)), COPY)
+        nc.sync.dma_start(out=out[:, :HALF], in_=res0[:])
+        nc.scalar.dma_start(out=out[:, HALF:], in_=res1[:])

@@ -17,7 +17,7 @@ P = 128
 PACK = 4
 HALF = SLOTS // 2
 LIST_HALF = HALF // 16
-N_MM = 256
+WIDTHS = (512, 256, 128, 128)
 
 FLOPS = 2 * D * T * Q
 
@@ -79,15 +79,17 @@ def tile_attend_middle_lean_through_heads_kernel(
         )
 
         a = keep.tile([P, T], F32, name="a")
-        for c in range(T // N_MM):
-            h, c0 = divmod(c * N_MM, T // 2)
-            cols = slice(c * N_MM, (c + 1) * N_MM)
-            bank = psum.tile([P, N_MM], F32, name="bank%d" % c)
+        start = 0
+        for c, width in enumerate(WIDTHS):
+            h, c0 = divmod(start, T // 2)
+            cols = slice(start, start + width)
+            start = start + width
+            bank = psum.tile([P, width], F32, name="bank%d" % c)
             nc.tensor.matmul_mx(
                 out=bank[:],
                 lhsT=q_codes[:].bitcast(FP8X4),
                 lhsT_scale=q_scales[:],
-                rhs=k_words[h][:, c0 : c0 + N_MM].bitcast(FP8X4),
+                rhs=k_words[h][:, c0 : c0 + width].bitcast(FP8X4),
                 rhs_scale=k_scales[:, cols],
                 start=True,
                 stop=True,
@@ -97,29 +99,28 @@ def tile_attend_middle_lean_through_heads_kernel(
             else:
                 nc.vector.tensor_copy(out=a[:, cols], in_=bank[:])
 
-        lam_wide = keep.tile([P, SLOTS], F32, name="lam_wide")
-        nc.gpsimd.tensor_copy(out=lam_wide[:], in_=lam_col[:].to_broadcast([P, SLOTS]))
-
         def half_of(lst, h):
             return lst[:, h * LIST_HALF : (h + 1) * LIST_HALF]
 
-        got = {}
+        first, others = [], []
         for h in range(2):
-            for n in range(3):
-                g = keep.tile([P, HALF], F32, name="got%d_%d" % (h, n))
-                if n == 0:
-                    nc.vector.tensor_copy(g[:], a[:].indirect(half_of(lists[n], h)))
-                else:
-                    nc.scalar.activation(g[:], a[:].indirect(half_of(lists[n], h)), COPY)
-                got[h, n] = g
+            first.append(keep.tile([P, HALF], F32, name="first%d" % h))
+            nc.vector.tensor_copy(first[h][:], a[:].indirect(half_of(lists[0], h)))
+            others.append(keep.tile([P, 2, HALF], F32, name="others%d" % h, tag="others%d" % h))
+            for n in range(2):
+                nc.scalar.activation(
+                    others[h][:, n, :], a[:].indirect(half_of(lists[1 + n], h)), COPY
+                )
         lo, cut = [], []
         for h in range(2):
             hi = keep.tile([P, HALF], F32, name="hi%d" % h)
             lo.append(keep.tile([P, HALF], F32, name="lo%d" % h))
             cut.append(keep.tile([P, HALF], F32, name="cut%d" % h))
-            nc.vector.tensor_tensor(hi[:], got[h, 0][:], got[h, 1][:], ALU.max)
-            nc.vector.tensor_tensor(lo[h][:], got[h, 0][:], got[h, 1][:], ALU.min)
-            nc.vector.tensor_tensor(cut[h][:], hi[:], got[h, 2][:], ALU.min)
+            nc.vector.tensor_tensor(hi[:], first[h][:], others[h][:, 0, :], ALU.max)
+            nc.vector.tensor_tensor(lo[h][:], first[h][:], others[h][:, 0, :], ALU.min)
+            nc.vector.tensor_tensor(cut[h][:], hi[:], others[h][:, 1, :], ALU.min)
+        lam_wide = keep.tile([P, SLOTS], F32, name="lam_wide", tag="others0")
+        nc.scalar.copy(out=lam_wide[:], in_=lam_col[:].to_broadcast([P, SLOTS]))
         med = keep.tile([P, SLOTS], F32, name="med")
         for h in range(2):
             nc.vector.tensor_tensor(med[:, h * HALF : (h + 1) * HALF], lo[h][:], cut[h][:], ALU.max)

@@ -1,6 +1,7 @@
 from contextlib import ExitStack
 
 import concourse.mybir as mybir
+from concourse.masks import make_identity
 
 F32 = mybir.dt.float32
 BF16 = mybir.dt.bfloat16
@@ -17,7 +18,10 @@ P = 128
 PACK = 4
 HALF = SLOTS // 2
 LIST_HALF = HALF // 16
-WIDTHS = (512, 256, 128, 128)
+WIDTHS = (256, 256, 256, 128, 128)
+KEY_LOADS = (256, 256, 512)
+V_COLS = 640
+Q_V = 88
 
 FLOPS = 2 * D * T * Q
 
@@ -39,11 +43,13 @@ def tile_attend_middle_lean_through_heads_kernel(
         words_hbm = keys_words[0].rearrange("p t r -> p (t r)").bitcast(I32)
         scales_hbm = keys_scales[0].bitcast(I32)
         k_words = []
-        for h in range(2):
-            w = keep.tile([P, T // 2], I32, name="k_words%d" % h, align_bytes=64)
-            nc.sync.dma_start(out=w[:], in_=words_hbm[:, h * (T // 2) : (h + 1) * (T // 2)])
-            k_words.append(w)
-            if h == 0:
+        start = 0
+        for n, width in enumerate(KEY_LOADS):
+            w = keep.tile([P, width], I32, name="k_words%d" % n, align_bytes=64)
+            nc.sync.dma_start(out=w[:], in_=words_hbm[:, start : start + width])
+            k_words.append((start, start + width, w))
+            start = start + width
+            if n == 0:
                 for quad in range(4):
                     nc.sync.dma_start(
                         out=k_scales[32 * quad : 32 * quad + 4, :].bitcast(I32),
@@ -67,8 +73,12 @@ def tile_attend_middle_lean_through_heads_kernel(
 
         q_bf = keep.tile([P, Q, PACK], BF16, name="q_bf", align_bytes=64)
         nc.vector.tensor_copy(
-            out=q_bf[:].rearrange("p (c i) j -> p c j i", i=4),
-            in_=q_raw[:].rearrange("p j (c i) -> p c j i", i=4),
+            out=q_bf[:, :Q_V, :].rearrange("p (c i) j -> p c j i", i=4),
+            in_=q_raw[:, :, :Q_V].rearrange("p j (c i) -> p c j i", i=4),
+        )
+        nc.scalar.copy(
+            out=q_bf[:, Q_V:, :].rearrange("p (c i) j -> p c j i", i=4),
+            in_=q_raw[:, :, Q_V:].rearrange("p j (c i) -> p c j i", i=4),
         )
         q_codes = keep.tile([P, Q], U32, name="q_codes", align_bytes=64)
         q_scales = keep.tile([P, Q], U8, name="q_scales", align_bytes=64)
@@ -81,15 +91,16 @@ def tile_attend_middle_lean_through_heads_kernel(
         a = keep.tile([P, T], F32, name="a")
         start = 0
         for c, width in enumerate(WIDTHS):
-            h, c0 = divmod(start, T // 2)
+            lo_col, words = [(b, w) for b, e, w in k_words if b <= start < e][0]
+            c0 = start - lo_col
             cols = slice(start, start + width)
             start = start + width
-            bank = psum.tile([P, width], F32, name="bank%d" % c)
+            bank = psum.tile([P, width], F32, name="bank%d" % c, tag="bank%d" % c)
             nc.tensor.matmul_mx(
                 out=bank[:],
                 lhsT=q_codes[:].bitcast(FP8X4),
                 lhsT_scale=q_scales[:],
-                rhs=k_words[h][:, c0 : c0 + width].bitcast(FP8X4),
+                rhs=words[:, c0 : c0 + width].bitcast(FP8X4),
                 rhs_scale=k_scales[:, cols],
                 start=True,
                 stop=True,
@@ -121,13 +132,29 @@ def tile_attend_middle_lean_through_heads_kernel(
             nc.vector.tensor_tensor(cut[h][:], hi[:], others[h][:, 1, :], ALU.min)
         lam_wide = keep.tile([P, SLOTS], F32, name="lam_wide", tag="others0")
         nc.scalar.copy(out=lam_wide[:], in_=lam_col[:].to_broadcast([P, SLOTS]))
+        ident = keep.tile([P, P], F32, name="ident")
+        make_identity(nc, ident[:])
+        old_banks = []
+        for n, c0 in enumerate(range(0, V_COLS, 512)):
+            width = min(512, V_COLS - c0)
+            turned = psum.tile([P, width], F32, name="turned%d" % n, tag="bank%d" % n)
+            for b in range(0, width, P):
+                nc.tensor.transpose(turned[:, b : b + P], old_sb[:, c0 + b : c0 + b + P], ident[:])
+            old_t = keep.tile([P, width], F32, name="old_t%d" % n)
+            nc.scalar.copy(out=old_t[:], in_=turned[:])
+            back = psum.tile([P, width], F32, name="back%d" % n)
+            for b in range(0, width, P):
+                nc.tensor.transpose(back[:, b : b + P], old_t[:, b : b + P], ident[:])
+            old_banks.append((slice(c0, c0 + width), back))
         med = keep.tile([P, SLOTS], F32, name="med")
         for h in range(2):
             nc.vector.tensor_tensor(med[:, h * HALF : (h + 1) * HALF], lo[h][:], cut[h][:], ALU.max)
         nc.vector.tensor_tensor(f1[:].indirect(lists[0][:]), med[:], lam_wide[:], ALU.mult)
 
         f2 = keep.tile([P, T], F32, name="f2")
-        nc.vector.tensor_tensor(f2[:], f1[:], old_sb[:], ALU.add)
+        for cols, bank in old_banks:
+            nc.vector.tensor_tensor(f2[:, cols], f1[:, cols], bank[:], ALU.add)
+        nc.gpsimd.tensor_tensor(f2[:, V_COLS:], f1[:, V_COLS:], old_sb[:, V_COLS:], ALU.add)
 
         res0 = keep.tile([P, HALF], F32, name="res0")
         res1 = keep.tile([P, HALF], F32, name="res1")

@@ -1,7 +1,6 @@
 from contextlib import ExitStack
 
 import concourse.mybir as mybir
-from concourse.masks import make_identity
 
 F32 = mybir.dt.float32
 BF16 = mybir.dt.bfloat16
@@ -19,9 +18,10 @@ PACK = 4
 HALF = SLOTS // 2
 LIST_HALF = HALF // 16
 WIDTHS = (256, 256, 256, 128, 128)
-KEY_LOADS = (256, 256, 512)
-V_COLS = 640
+KEY_LOADS = (512, 512)
+
 Q_V = 88
+QUARTER = T // 4
 
 FLOPS = 2 * D * T * Q
 
@@ -34,14 +34,14 @@ def tile_attend_middle_lean_through_heads_kernel(
         keep = ctx.enter_context(tc.tile_pool(name="keep", bufs=1))
         psum = ctx.enter_context(tc.psum_pool(name="psum", bufs=1))
 
-        k_scales = keep.tile([P, T], U8, name="k_scales", align_bytes=64)
+        k_scales = keep.tile([P, QUARTER], U8, name="k_scales", align_bytes=64)
         nc.vector.memset(k_scales[:].bitcast(I32), 0)
 
         q_raw = keep.tile([P, PACK, Q], F32, name="q_raw")
         nc.sync.dma_start(out=q_raw[:], in_=query.rearrange("(p j) q -> p j q", j=PACK))
 
         words_hbm = keys_words[0].rearrange("p t r -> p (t r)").bitcast(I32)
-        scales_hbm = keys_scales[0].bitcast(I32)
+        scales_hbm = keys_scales[0].bitcast(I32).rearrange("f (u w) -> u f w", u=4)
         k_words = []
         start = 0
         for n, width in enumerate(KEY_LOADS):
@@ -52,8 +52,8 @@ def tile_attend_middle_lean_through_heads_kernel(
             if n == 0:
                 for quad in range(4):
                     nc.sync.dma_start(
-                        out=k_scales[32 * quad : 32 * quad + 4, :].bitcast(I32),
-                        in_=scales_hbm[4 * quad : 4 * quad + 4, :],
+                        out=k_scales[32 * quad : 32 * quad + 16, :].bitcast(I32),
+                        in_=scales_hbm[:, 4 * quad : 4 * quad + 4, :],
                     )
 
         lists = []
@@ -93,15 +93,16 @@ def tile_attend_middle_lean_through_heads_kernel(
         for c, width in enumerate(WIDTHS):
             lo_col, words = [(b, w) for b, e, w in k_words if b <= start < e][0]
             c0 = start - lo_col
+            u, s0 = divmod(start, QUARTER)
             cols = slice(start, start + width)
             start = start + width
-            bank = psum.tile([P, width], F32, name="bank%d" % c, tag="bank%d" % c)
+            bank = psum.tile([P, width], F32, name="bank%d" % c)
             nc.tensor.matmul_mx(
                 out=bank[:],
                 lhsT=q_codes[:].bitcast(FP8X4),
                 lhsT_scale=q_scales[:],
                 rhs=words[:, c0 : c0 + width].bitcast(FP8X4),
-                rhs_scale=k_scales[:, cols],
+                rhs_scale=k_scales[4 * u :, s0 : s0 + width],
                 start=True,
                 stop=True,
             )
@@ -132,29 +133,13 @@ def tile_attend_middle_lean_through_heads_kernel(
             nc.vector.tensor_tensor(cut[h][:], hi[:], others[h][:, 1, :], ALU.min)
         lam_wide = keep.tile([P, SLOTS], F32, name="lam_wide", tag="others0")
         nc.scalar.copy(out=lam_wide[:], in_=lam_col[:].to_broadcast([P, SLOTS]))
-        ident = keep.tile([P, P], F32, name="ident")
-        make_identity(nc, ident[:])
-        old_banks = []
-        for n, c0 in enumerate(range(0, V_COLS, 512)):
-            width = min(512, V_COLS - c0)
-            turned = psum.tile([P, width], F32, name="turned%d" % n, tag="bank%d" % n)
-            for b in range(0, width, P):
-                nc.tensor.transpose(turned[:, b : b + P], old_sb[:, c0 + b : c0 + b + P], ident[:])
-            old_t = keep.tile([P, width], F32, name="old_t%d" % n)
-            nc.scalar.copy(out=old_t[:], in_=turned[:])
-            back = psum.tile([P, width], F32, name="back%d" % n)
-            for b in range(0, width, P):
-                nc.tensor.transpose(back[:, b : b + P], old_t[:, b : b + P], ident[:])
-            old_banks.append((slice(c0, c0 + width), back))
         med = keep.tile([P, SLOTS], F32, name="med")
         for h in range(2):
             nc.vector.tensor_tensor(med[:, h * HALF : (h + 1) * HALF], lo[h][:], cut[h][:], ALU.max)
         nc.vector.tensor_tensor(f1[:].indirect(lists[0][:]), med[:], lam_wide[:], ALU.mult)
 
         f2 = keep.tile([P, T], F32, name="f2")
-        for cols, bank in old_banks:
-            nc.vector.tensor_tensor(f2[:, cols], f1[:, cols], bank[:], ALU.add)
-        nc.gpsimd.tensor_tensor(f2[:, V_COLS:], f1[:, V_COLS:], old_sb[:, V_COLS:], ALU.add)
+        nc.vector.tensor_tensor(f2[:], f1[:], old_sb[:], ALU.add)
 
         res0 = keep.tile([P, HALF], F32, name="res0")
         res1 = keep.tile([P, HALF], F32, name="res1")

from contextlib import ExitStack

import concourse.mybir as mybir

F32 = mybir.dt.float32
BF16 = mybir.dt.bfloat16
I32 = mybir.dt.int32
U32 = mybir.dt.uint32
U16 = mybir.dt.uint16
U8 = mybir.dt.uint8
FP8X4 = mybir.dt.float8_e4m3fn_x4
ALU = mybir.AluOpType
COPY = mybir.ActivationFunctionType.Copy

D, T, SLOTS, Q = 512, 1024, 512, 128
P = 128
PACK = 4
HALF = SLOTS // 2
LIST_HALF = HALF // 16
WIDTHS = (256, 256, 256, 128, 128)
KEY_LOADS = (512, 512)

Q_V = 88
QUARTER = T // 4

FLOPS = 2 * D * T * Q


def tile_attend_middle_lean_through_heads_kernel(
    tc, query, keys_words, keys_scales, lam, old, offs, offs2, offs3, offs4, out
):
    nc = tc.nc
    with ExitStack() as ctx:
        keep = ctx.enter_context(tc.tile_pool(name="keep", bufs=1))
        psum = ctx.enter_context(tc.psum_pool(name="psum", bufs=1))

        k_scales = keep.tile([P, QUARTER], U8, name="k_scales", align_bytes=64)
        nc.vector.memset(k_scales[:].bitcast(I32), 0)

        q_raw = keep.tile([P, PACK, Q], F32, name="q_raw")
        nc.sync.dma_start(out=q_raw[:], in_=query.rearrange("(p j) q -> p j q", j=PACK))

        words_hbm = keys_words[0].rearrange("p t r -> p (t r)").bitcast(I32)
        scales_hbm = keys_scales[0].bitcast(I32).rearrange("f (u w) -> u f w", u=4)
        k_words = []
        start = 0
        for n, width in enumerate(KEY_LOADS):
            w = keep.tile([P, width], I32, name="k_words%d" % n, align_bytes=64)
            nc.sync.dma_start(out=w[:], in_=words_hbm[:, start : start + width])
            k_words.append((start, start + width, w))
            start = start + width
            if n == 0:
                for quad in range(4):
                    nc.sync.dma_start(
                        out=k_scales[32 * quad : 32 * quad + 16, :].bitcast(I32),
                        in_=scales_hbm[:, 4 * quad : 4 * quad + 4, :],
                    )

        lists = []
        for n, src in enumerate((offs, offs2, offs3)):
            lst = keep.tile([P, SLOTS // 16], U16, name="list%d" % n)
            nc.sync.dma_start(lst[:], src)
            lists.append(lst)
        lam_col = keep.tile([P, 1], F32, name="lam_col")
        nc.sync.dma_start(out=lam_col[:], in_=lam)
        list_out = keep.tile([P, SLOTS // 16], U16, name="list_out")
        nc.sync.dma_start(list_out[:], offs4)
        old_sb = keep.tile([P, T], F32, name="old_sb")
        nc.sync.dma_start(out=old_sb[:], in_=old)

        f1 = keep.tile([P, T], F32, name="f1")
        nc.vector.memset(f1[:], 0.0)

        q_bf = keep.tile([P, Q, PACK], BF16, name="q_bf", align_bytes=64)
        nc.vector.tensor_copy(
            out=q_bf[:, :Q_V, :].rearrange("p (c i) j -> p c j i", i=4),
            in_=q_raw[:, :, :Q_V].rearrange("p j (c i) -> p c j i", i=4),
        )
        nc.scalar.copy(
            out=q_bf[:, Q_V:, :].rearrange("p (c i) j -> p c j i", i=4),
            in_=q_raw[:, :, Q_V:].rearrange("p j (c i) -> p c j i", i=4),
        )
        q_codes = keep.tile([P, Q], U32, name="q_codes", align_bytes=64)
        q_scales = keep.tile([P, Q], U8, name="q_scales", align_bytes=64)
        nc.vector.quantize_mx(
            out=q_codes[:].bitcast(FP8X4),
            scales=q_scales[:],
            in_=q_bf[:].rearrange("p q j -> p (q j)"),
        )

        a = keep.tile([P, T], F32, name="a")
        start = 0
        for c, width in enumerate(WIDTHS):
            lo_col, words = [(b, w) for b, e, w in k_words if b <= start < e][0]
            c0 = start - lo_col
            u, s0 = divmod(start, QUARTER)
            cols = slice(start, start + width)
            start = start + width
            bank = psum.tile([P, width], F32, name="bank%d" % c)
            nc.tensor.matmul_mx(
                out=bank[:],
                lhsT=q_codes[:].bitcast(FP8X4),
                lhsT_scale=q_scales[:],
                rhs=words[:, c0 : c0 + width].bitcast(FP8X4),
                rhs_scale=k_scales[4 * u :, s0 : s0 + width],
                start=True,
                stop=True,
            )
            if c % 2 == 0:
                nc.scalar.copy(out=a[:, cols], in_=bank[:])
            else:
                nc.vector.tensor_copy(out=a[:, cols], in_=bank[:])

        def half_of(lst, h):
            return lst[:, h * LIST_HALF : (h + 1) * LIST_HALF]

        first, others = [], []
        for h in range(2):
            first.append(keep.tile([P, HALF], F32, name="first%d" % h))
            nc.vector.tensor_copy(first[h][:], a[:].indirect(half_of(lists[0], h)))
            others.append(keep.tile([P, 2, HALF], F32, name="others%d" % h, tag="others%d" % h))
            for n in range(2):
                nc.scalar.activation(
                    others[h][:, n, :], a[:].indirect(half_of(lists[1 + n], h)), COPY
                )
        lo, cut = [], []
        for h in range(2):
            hi = keep.tile([P, HALF], F32, name="hi%d" % h)
            lo.append(keep.tile([P, HALF], F32, name="lo%d" % h))
            cut.append(keep.tile([P, HALF], F32, name="cut%d" % h))
            nc.vector.tensor_tensor(hi[:], first[h][:], others[h][:, 0, :], ALU.max)
            nc.vector.tensor_tensor(lo[h][:], first[h][:], others[h][:, 0, :], ALU.min)
            nc.vector.tensor_tensor(cut[h][:], hi[:], others[h][:, 1, :], ALU.min)
        lam_wide = keep.tile([P, SLOTS], F32, name="lam_wide", tag="others0")
        nc.scalar.copy(out=lam_wide[:], in_=lam_col[:].to_broadcast([P, SLOTS]))
        med = keep.tile([P, SLOTS], F32, name="med")
        for h in range(2):
            nc.vector.tensor_tensor(med[:, h * HALF : (h + 1) * HALF], lo[h][:], cut[h][:], ALU.max)
        nc.vector.tensor_tensor(f1[:].indirect(lists[0][:]), med[:], lam_wide[:], ALU.mult)

        f2 = keep.tile([P, T], F32, name="f2")
        nc.vector.tensor_tensor(f2[:], f1[:], old_sb[:], ALU.add)

        res0 = keep.tile([P, HALF], F32, name="res0")
        res1 = keep.tile([P, HALF], F32, name="res1")
        nc.vector.tensor_copy(res0[:], f2[:].indirect(half_of(list_out, 0)))
        nc.scalar.activation(res1[:], f2[:].indirect(half_of(list_out, 1)), COPY)
        nc.sync.dma_start(out=out[:, :HALF], in_=res0[:])
        nc.scalar.dma_start(out=out[:, HALF:], in_=res1[:])
